import numpy as np
import ml_dtypes


def mxq(x, axis, fmt="e4m3"):
    dtype, down = {"e4m3": (ml_dtypes.float8_e4m3fn, 7), "e5m2": (ml_dtypes.float8_e5m2, 14)}[fmt]
    v = np.moveaxis(np.asarray(x, np.float32).astype(ml_dtypes.bfloat16).astype(np.float64), axis, -1)
    blocks = v.reshape(v.shape[:-1] + (-1, 32))
    amax = np.abs(blocks).max(-1, keepdims=True)
    byte = np.maximum(np.where(amax > 0, np.frexp(amax)[1] - 1 + 127, 0) - down, 1)
    scale = np.exp2(byte - 127.0)
    codes = (blocks / scale).astype(np.float32).astype(dtype).astype(np.float64)
    return np.moveaxis((codes * scale).reshape(v.shape), -1, axis)


WIDE = False


def mx_kscale(k):
    if not WIDE:
        return np.ones(k)
    levels = np.array([10, -10, 5, -5, 0])
    if k % 512:
        return np.exp2(np.random.permutation(np.resize(levels, k // 32))).repeat(32)
    a = np.empty((k // 512, 16))
    for p in range(k // 512):
        a[p, :8] = np.random.permutation(np.resize(levels, 8))
        for g in range(8):
            far = levels[np.abs(levels - a[p, g]) >= 10]
            a[p, g + 8] = far[np.random.randint(len(far))]
    return np.exp2(a.ravel()).repeat(32)


def f64(x):
    return np.asarray(x).astype(np.float64)


def striped(idx):
    return np.tile(idx.reshape(-1, 16).T, (8, 1)).astype(np.uint16)


def unstriped(offs):
    return offs[:16].T.reshape(-1).astype(np.int64)


def pack_weight(w):
    k, n = w.shape
    w = f64(np.asarray(w, np.float32).astype(ml_dtypes.bfloat16)).reshape(k // 32, 32, n)
    amax = np.abs(w).max(1)
    byte = np.clip(np.where(amax > 0, np.frexp(amax)[1] - 1 + 127 - 7, 1), 1, 254)
    scaled = (w * np.exp2(127.0 - byte)[:, None, :]).reshape(k, n).astype(np.float32)
    words = np.ascontiguousarray(scaled.reshape(k // 512, 128, 4, n).transpose(0, 1, 3, 2)).astype(ml_dtypes.float8_e4m3fn).view(np.uint8)
    return words, np.ascontiguousarray(byte.astype(np.uint8).reshape(k // 512, 16, n))


def unpack_weight(words, scales):
    g, p, n, _ = words.shape
    vals = np.ascontiguousarray(words).view(ml_dtypes.float8_e4m3fn).astype(np.float64) * np.repeat(np.exp2(scales.astype(np.float64) - 127.0), 8, axis=1)[..., None]
    return vals.transpose(0, 1, 3, 2).reshape(g * 512, n)


K, T, S, V = 512, 1024, 512, 512
P = 2 ** 7


def setup_inputs():
    n = np.random.standard_normal
    s = mx_kscale(K)[:, None]
    packed_xT = pack_weight(n((K, T)) * s)
    return {
        "x_words": packed_xT[0],
        "x_scales": packed_xT[1],
        "hT": (n((K, V)) / np.sqrt(K) / s).astype(np.float32),
        "prev": (np.random.uniform(0.0, 3.0, (V, S))).astype(np.float32),
        "jump": (np.tile(np.random.uniform(1.0, 1.4, S), (P, 1))).astype(np.float32),
        "offs": striped(np.random.permutation(T)[:S]),
    }


def reference(x_words, x_scales, hT, prev, jump, offs):
    hTq = mxq(f64(hT), 0, "e4m3")
    xq = unpack_weight(x_words, x_scales)[:, unstriped(offs)]
    cst = -0.3 * (hTq.T @ xq) + 1.0
    mn = f64(prev).min(axis=1, keepdims=True)
    lq = f64(prev) - mn
    iv = -1.0 * lq + 5.0
    side = np.maximum(np.pad(iv, ((0, 0), (1, 0)))[:, :S], np.pad(iv, ((0, 0), (0, 1)))[:, 1:])
    ww = -3.0 * (cst + np.minimum(np.minimum(lq, -1.0 * side + 5.3), f64(jump)[:1]))
    ex = np.exp(ww - ww.max(axis=1, keepdims=True))
    return ex / ex.sum(axis=1, keepdims=True)

@@ -1,0 +1,135 @@
+from contextlib import ExitStack
+
+import concourse.mybir as mybir
+
+K, T, S, V = 512, 1024, 512, 512
+P = 128
+PACK = 4
+TILES = V // P
+PAD = 8
+FLOPS = 2 * K * S * V
+FLOAT_MAX = 3.4028234663852886e38
+
+F32 = mybir.dt.float32
+BF16 = mybir.dt.bfloat16
+I32 = mybir.dt.int32
+U32 = mybir.dt.uint32
+U16 = mybir.dt.uint16
+U8 = mybir.dt.uint8
+FP8X4 = mybir.dt.float8_e4m3fn_x4
+ALU = mybir.AluOpType
+ACT = mybir.ActivationFunctionType
+AX = mybir.AxisListType
+
+
+def tile_picked_ysgm_soft_p_kernel(tc, x_words, x_scales, hT, prev, jump, offs, out):
+    nc = tc.nc
+    with ExitStack() as ctx:
+        keep = ctx.enter_context(tc.tile_pool(name="keep", bufs=1))
+        psum = ctx.enter_context(tc.psum_pool(name="psum", bufs=1))
+
+        offsets = keep.tile([P, S // 16], U16, name="offsets")
+        table_words = keep.tile([P, T], U32, name="table_words", align_bytes=64)
+        table_scales = keep.tile([P, T], U8, name="table_scales", align_bytes=64)
+        x_codes = keep.tile([P, S], U32, name="x_codes", align_bytes=64)
+        x_bytes = keep.tile([P, S], U8, name="x_bytes", align_bytes=64)
+        prev_t = [keep.tile([P, S + 2 * PAD], F32, name=f"prev{i}") for i in range(TILES)]
+        jump_t = keep.tile([P, S], F32, name="jump_t")
+        half = V // 2
+        h_raw = [keep.tile([P, PACK, half], F32, name=f"h_raw{u}") for u in range(2)]
+        h_bf = [keep.tile([P, half * PACK], BF16, name=f"h_bf{u}", align_bytes=64) for u in range(2)]
+        h_codes = [keep.tile([P, half], U32, name=f"h_codes{u}", align_bytes=64) for u in range(2)]
+        h_bytes = [keep.tile([P, half], U8, name=f"h_bytes{u}", align_bytes=64) for u in range(2)]
+        warm = keep.tile([P, 2], F32, name="warm")
+
+        nc.vector.memset(table_scales[:].bitcast(I32), 0)
+        nc.vector.memset(warm[:, 0:1], 0.0)
+        nc.scalar.activation(warm[:, 1:2], warm[:, 0:1], ACT.Exp)
+        for i in range(TILES):
+            nc.gpsimd.memset(prev_t[i][:, PAD - 1 : PAD], FLOAT_MAX)
+            nc.gpsimd.memset(prev_t[i][:, PAD + S : PAD + S + 1], FLOAT_MAX)
+
+        h_view = hT.rearrange("(p j) w -> p j w", j=PACK)
+        scale_rows = x_scales[0].bitcast(I32)
+
+        def load_prev(i):
+            nc.sync.dma_start(prev_t[i][:, PAD : PAD + S], prev[i * P : (i + 1) * P, :])
+
+        load_prev(0)
+        nc.sync.dma_start(offsets[:], offs)
+        nc.sync.dma_start(table_words[:].bitcast(I32), x_words[0].rearrange("p n t -> p (n t)").bitcast(I32))
+        for q in range(4):
+            nc.sync.dma_start(table_scales[32 * q : 32 * q + 4, :].bitcast(I32), scale_rows[4 * q : 4 * q + 4, :])
+        nc.sync.dma_start(jump_t[:], jump)
+        nc.sync.dma_start(h_raw[0][:], h_view[:, :, 0:half])
+        load_prev(1)
+        nc.sync.dma_start(h_raw[1][:], h_view[:, :, half:V])
+        load_prev(2)
+        load_prev(3)
+
+        ends = jump_t[:, 0 : S : S - 1]
+        nc.gpsimd.tensor_scalar(ends, ends, 5.3, None, ALU.min)
+
+        stats = keep.tile([P, 4 * TILES], F32, name="stats")
+        sums = keep.tile([P, TILES], F32, name="sums")
+        pen = []
+
+        def penalty(i):
+            p = prev_t[i]
+            near = keep.tile([P, S], F32, name=f"near{i}")
+            nc.vector.tensor_tensor(near[:], p[:, PAD - 1 : PAD - 1 + S], p[:, PAD + 1 : PAD + 1 + S], ALU.min)
+            mn = stats[:, i : i + 1]
+            nc.vector.tensor_reduce(mn, near[:].rearrange("p (a b) -> p a b", b=4)[:, :, 1:3], AX.XY, ALU.min)
+            stay = keep.tile([P, S], F32, name=f"stay{i}")
+            nc.vector.scalar_tensor_tensor(stay[:], near[:], 0.3, p[:, PAD : PAD + S], ALU.add, ALU.min)
+            m = keep.tile([P, S], F32, name=f"pen{i}")
+            nc.vector.scalar_tensor_tensor(m[:], stay[:], mn, jump_t[:], ALU.subtract, ALU.min)
+            pen.append(m)
+
+        def quantise(u):
+            nc.scalar.copy(
+                h_bf[u][:].rearrange("p (c i t) -> p c t i", i=4, t=PACK),
+                h_raw[u][:].rearrange("p t (c i) -> p c t i", i=4),
+            )
+            nc.vector.quantize_mx(out=h_codes[u][:].bitcast(FP8X4), scales=h_bytes[u][:], in_=h_bf[u][:])
+
+        def finish(i):
+            u, c = divmod(i, 2)
+            acc = psum.tile([P, S], F32, name=f"acc{i}")
+            nc.tensor.matmul_mx(
+                out=acc[:],
+                lhsT=h_codes[u][:, c * P : (c + 1) * P].bitcast(FP8X4),
+                lhsT_scale=h_bytes[u][:, c * P : (c + 1) * P],
+                rhs=x_codes[:].bitcast(FP8X4),
+                rhs_scale=x_bytes[:],
+                start=True,
+                stop=True,
+            )
+            z = keep.tile([P, S], F32, name=f"z{i}")
+            nc.vector.scalar_tensor_tensor(z[:], acc[:], 0.3, pen[i][:], ALU.mult, ALU.subtract)
+            cost = keep.tile([P, S], F32, name=f"cost{i}")
+            low = stats[:, TILES + i : TILES + i + 1]
+            nc.vector.tensor_scalar(cost[:], z[:], -3.0, None, ALU.mult, ALU.min, accum_out=low)
+            e = keep.tile([P, S], F32, name=f"e{i}")
+            nc.scalar.activation(e[:], cost[:], ACT.Exp, bias=low, scale=-1.0, accum_out=sums[:, i : i + 1])
+            r = stats[:, 2 * TILES + i : 2 * TILES + i + 1]
+            nc.vector.reciprocal(r, sums[:, i : i + 1])
+            o = keep.tile([P, S], F32, name=f"o{i}")
+            if i == TILES - 1:
+                nc.vector.tensor_scalar(o[:], e[:], r, None, ALU.mult)
+            else:
+                nc.scalar.activation(o[:], e[:], ACT.Copy, scale=r)
+            nc.sync.dma_start(out[i * P : (i + 1) * P, :], o[:])
+
+        penalty(0)
+        nc.vector.tensor_copy(x_codes[:], table_words[:].indirect(offsets[:]))
+        nc.vector.tensor_copy(x_bytes[:], table_scales[:].indirect(offsets[:]))
+        quantise(0)
+        penalty(1)
+        quantise(1)
+        finish(0)
+        penalty(2)
+        finish(1)
+        penalty(3)
+        finish(2)
+        finish(3)

@@ -1,11 +1,13 @@
 from contextlib import ExitStack
 
 import concourse.mybir as mybir
+from concourse.masks import make_identity
 
 K, T, S, V = 512, 1024, 512, 512
 P = 128
 PACK = 4
 TILES = V // P
+BLOCKS = S // P
 PAD = 8
 FLOPS = 2 * K * S * V
 FLOAT_MAX = 3.4028234663852886e38
@@ -26,7 +28,7 @@ def tile_picked_ysgm_soft_p_kernel(tc, x_words, x_scales, hT, prev, jump, offs, 
     nc = tc.nc
     with ExitStack() as ctx:
         keep = ctx.enter_context(tc.tile_pool(name="keep", bufs=1))
-        psum = ctx.enter_context(tc.psum_pool(name="psum", bufs=1))
+        psum = ctx.enter_context(tc.psum_pool(name="psum", bufs=2))
 
         offsets = keep.tile([P, S // 16], U16, name="offsets")
         table_words = keep.tile([P, T], U32, name="table_words", align_bytes=64)
@@ -34,20 +36,30 @@ def tile_picked_ysgm_soft_p_kernel(tc, x_words, x_scales, hT, prev, jump, offs, 
         x_codes = keep.tile([P, S], U32, name="x_codes", align_bytes=64)
         x_bytes = keep.tile([P, S], U8, name="x_bytes", align_bytes=64)
         prev_t = [keep.tile([P, S + 2 * PAD], F32, name=f"prev{i}") for i in range(TILES)]
-        jump_t = keep.tile([P, S], F32, name="jump_t")
+        jump_rows = keep.tile([P, P], F32, name="jump_rows")
         half = V // 2
         h_raw = [keep.tile([P, PACK, half], F32, name=f"h_raw{u}") for u in range(2)]
-        h_bf = [keep.tile([P, half * PACK], BF16, name=f"h_bf{u}", align_bytes=64) for u in range(2)]
+        h_bf = [keep.tile([P, half * PACK], BF16, name=f"h_bf{u}", tag=f"work{u + 1}", align_bytes=64) for u in range(2)]
         h_codes = [keep.tile([P, half], U32, name=f"h_codes{u}", align_bytes=64) for u in range(2)]
         h_bytes = [keep.tile([P, half], U8, name=f"h_bytes{u}", align_bytes=64) for u in range(2)]
         warm = keep.tile([P, 2], F32, name="warm")
+        ident = keep.tile([P, P], F32, name="ident")
+        cap = keep.tile([P, BLOCKS], F32, name="cap")
+        jump3 = keep.tile([P, BLOCKS], F32, name="jump3")
+        jump3_neg = keep.tile([P, BLOCKS], F32, name="jump3_neg")
 
-        nc.vector.memset(table_scales[:].bitcast(I32), 0)
+        nc.gpsimd.memset(table_scales[:].bitcast(I32), 0)
+        nc.gpsimd.memset(jump_rows[:], 0.0)
         nc.vector.memset(warm[:, 0:1], 0.0)
         nc.scalar.activation(warm[:, 1:2], warm[:, 0:1], ACT.Exp)
         for i in range(TILES):
             nc.gpsimd.memset(prev_t[i][:, PAD - 1 : PAD], FLOAT_MAX)
             nc.gpsimd.memset(prev_t[i][:, PAD + S : PAD + S + 1], FLOAT_MAX)
+        make_identity(nc, ident[:])
+        nc.gpsimd.memset(cap[:, 1 : BLOCKS - 1], FLOAT_MAX)
+        cap_ends = cap[:, 0 : BLOCKS : BLOCKS - 1]
+        nc.gpsimd.tensor_scalar(cap_ends, ident[:, 0 : P : P - 1], -FLOAT_MAX, FLOAT_MAX, ALU.mult, ALU.add)
+        nc.gpsimd.tensor_scalar(cap_ends, cap_ends, 3 * 5.3, 1.0, ALU.add, ALU.mult)
 
         h_view = hT.rearrange("(p j) w -> p j w", j=PACK)
         scale_rows = x_scales[0].bitcast(I32)
@@ -60,76 +72,96 @@ def tile_picked_ysgm_soft_p_kernel(tc, x_words, x_scales, hT, prev, jump, offs, 
         nc.sync.dma_start(table_words[:].bitcast(I32), x_words[0].rearrange("p n t -> p (n t)").bitcast(I32))
         for q in range(4):
             nc.sync.dma_start(table_scales[32 * q : 32 * q + 4, :].bitcast(I32), scale_rows[4 * q : 4 * q + 4, :])
-        nc.sync.dma_start(jump_t[:], jump)
         nc.sync.dma_start(h_raw[0][:], h_view[:, :, 0:half])
+        nc.sync.dma_start(jump_rows[0:BLOCKS, :], jump[0, :].rearrange("(c p) -> c p", p=P))
         load_prev(1)
-        nc.sync.dma_start(h_raw[1][:], h_view[:, :, half:V])
         load_prev(2)
+        nc.sync.dma_start(h_raw[1][:], h_view[:, :, half:V])
         load_prev(3)
 
-        ends = jump_t[:, 0 : S : S - 1]
-        nc.gpsimd.tensor_scalar(ends, ends, 5.3, None, ALU.min)
+        jump_cols = psum.tile([P, S], F32, name="turned")
+        nc.tensor.transpose(jump_cols[:, 0:P], jump_rows[:], ident[:])
+        nc.vector.scalar_tensor_tensor(jump3[:], jump_cols[:, 0:BLOCKS], 3.0, cap[:], ALU.mult, ALU.min)
+        nc.scalar.mul(jump3_neg[:], jump3[:], -1.0)
 
         stats = keep.tile([P, 4 * TILES], F32, name="stats")
         sums = keep.tile([P, TILES], F32, name="sums")
-        pen = []
+        gain = []
+        base = [keep.tile([P, BLOCKS, half], F32, name=f"base{u}") for u in range(2)]
 
         def penalty(i):
             p = prev_t[i]
-            near = keep.tile([P, S], F32, name=f"near{i}")
+            near = keep.tile([P, S], F32, name=f"near{i}", tag=f"work{i}", align_bytes=64)
             nc.vector.tensor_tensor(near[:], p[:, PAD - 1 : PAD - 1 + S], p[:, PAD + 1 : PAD + 1 + S], ALU.min)
-            mn = stats[:, i : i + 1]
-            nc.vector.tensor_reduce(mn, near[:].rearrange("p (a b) -> p a b", b=4)[:, :, 1:3], AX.XY, ALU.min)
+            neg_mn = stats[:, i : i + 1]
+            nc.vector.tensor_reduce(neg_mn, near[:].rearrange("p (a b) -> p a b", b=4)[:, :, 1:3], AX.XY, ALU.min, negate=True)
             stay = keep.tile([P, S], F32, name=f"stay{i}")
             nc.vector.scalar_tensor_tensor(stay[:], near[:], 0.3, p[:, PAD : PAD + S], ALU.add, ALU.min)
-            m = keep.tile([P, S], F32, name=f"pen{i}")
-            nc.vector.scalar_tensor_tensor(m[:], stay[:], mn, jump_t[:], ALU.subtract, ALU.min)
-            pen.append(m)
+            turned = psum.tile([P, S], F32, name="turned")
+            for c in range(BLOCKS):
+                cols = slice(c * P, (c + 1) * P)
+                nc.tensor.matmul(turned[:, cols], neg_mn.to_broadcast([P, P]), ident[:], start=(c == 0), stop=False, is_transpose=True)
+            for c in range(BLOCKS):
+                cols = slice(c * P, (c + 1) * P)
+                nc.tensor.matmul(turned[:, cols], stay[:, cols], ident[:], start=False, stop=(c == BLOCKS - 1), is_transpose=True)
+            w = keep.tile([P, S], F32, name=f"gain{i}")
+            for c in range(BLOCKS):
+                cols = slice(c * P, (c + 1) * P)
+                nc.scalar.activation(w[:, cols], turned[:, cols], ACT.Relu, bias=jump3[:, c : c + 1], scale=-3.0)
+            gain.append(w)
 
-        def quantise(u):
+        def product(u):
             nc.scalar.copy(
                 h_bf[u][:].rearrange("p (c i t) -> p c t i", i=4, t=PACK),
                 h_raw[u][:].rearrange("p t (c i) -> p c t i", i=4),
             )
             nc.vector.quantize_mx(out=h_codes[u][:].bitcast(FP8X4), scales=h_bytes[u][:], in_=h_bf[u][:])
+            for pair in range(BLOCKS // 2):
+                acc = psum.tile([P, 2, half], F32, name="acc", bufs=2)
+                for d in range(2):
+                    c = 2 * pair + d
+                    nc.tensor.matmul_mx(
+                        out=acc[:, d, :],
+                        lhsT=x_codes[:, c * P : (c + 1) * P].bitcast(FP8X4),
+                        lhsT_scale=x_bytes[:, c * P : (c + 1) * P],
+                        rhs=h_codes[u][:].bitcast(FP8X4),
+                        rhs_scale=h_bytes[u][:],
+                        start=True,
+                        stop=True,
+                    )
+                for d in range(2):
+                    c = 2 * pair + d
+                    nc.scalar.activation(base[u][:, c, :], acc[:, d, :], ACT.Identity, bias=jump3_neg[:, c : c + 1], scale=0.9)
 
         def finish(i):
-            u, c = divmod(i, 2)
-            acc = psum.tile([P, S], F32, name=f"acc{i}")
-            nc.tensor.matmul_mx(
-                out=acc[:],
-                lhsT=h_codes[u][:, c * P : (c + 1) * P].bitcast(FP8X4),
-                lhsT_scale=h_bytes[u][:, c * P : (c + 1) * P],
-                rhs=x_codes[:].bitcast(FP8X4),
-                rhs_scale=x_bytes[:],
-                start=True,
-                stop=True,
-            )
-            z = keep.tile([P, S], F32, name=f"z{i}")
-            nc.vector.scalar_tensor_tensor(z[:], acc[:], 0.3, pen[i][:], ALU.mult, ALU.subtract)
-            cost = keep.tile([P, S], F32, name=f"cost{i}")
-            low = stats[:, TILES + i : TILES + i + 1]
-            nc.vector.tensor_scalar(cost[:], z[:], -3.0, None, ALU.mult, ALU.min, accum_out=low)
+            u, d = divmod(i, 2)
+            z = psum.tile([P, S], F32, name="z", bufs=4)
+            for c in range(BLOCKS):
+                cols = slice(c * P, (c + 1) * P)
+                nc.tensor.matmul(z[:, cols], base[u][:, c, d * P : (d + 1) * P], ident[:], start=(c == 0), stop=False, is_transpose=True)
+            for c in range(BLOCKS):
+                cols = slice(c * P, (c + 1) * P)
+                nc.tensor.matmul(z[:, cols], gain[i][:, cols], ident[:], start=False, stop=(c == BLOCKS - 1), is_transpose=True)
+            neg_max = stats[:, TILES + i : TILES + i + 1]
+            nc.vector.tensor_reduce(neg_max, z[:], AX.X, ALU.max, negate=True)
             e = keep.tile([P, S], F32, name=f"e{i}")
-            nc.scalar.activation(e[:], cost[:], ACT.Exp, bias=low, scale=-1.0, accum_out=sums[:, i : i + 1])
+            nc.scalar.activation(e[:], z[:], ACT.Exp, bias=neg_max, accum_out=sums[:, i : i + 1])
             r = stats[:, 2 * TILES + i : 2 * TILES + i + 1]
             nc.vector.reciprocal(r, sums[:, i : i + 1])
             o = keep.tile([P, S], F32, name=f"o{i}")
             if i == TILES - 1:
                 nc.vector.tensor_scalar(o[:], e[:], r, None, ALU.mult)
             else:
-                nc.scalar.activation(o[:], e[:], ACT.Copy, scale=r)
+                nc.gpsimd.tensor_scalar(o[:], e[:], r, 1.0, ALU.mult, ALU.mult)
             nc.sync.dma_start(out[i * P : (i + 1) * P, :], o[:])
 
         penalty(0)
         nc.vector.tensor_copy(x_codes[:], table_words[:].indirect(offsets[:]))
         nc.vector.tensor_copy(x_bytes[:], table_scales[:].indirect(offsets[:]))
-        quantise(0)
+        product(0)
         penalty(1)
-        quantise(1)
-        finish(0)
+        product(1)
         penalty(2)
-        finish(1)
         penalty(3)
-        finish(2)
-        finish(3)
+        for i in range(TILES):
+            finish(i)

@@ -39,27 +39,28 @@ def tile_picked_ysgm_soft_p_kernel(tc, x_words, x_scales, hT, prev, jump, offs, 
         jump_rows = keep.tile([P, P], F32, name="jump_rows")
         half = V // 2
         h_raw = [keep.tile([P, PACK, half], F32, name=f"h_raw{u}") for u in range(2)]
-        h_bf = [keep.tile([P, half * PACK], BF16, name=f"h_bf{u}", tag=f"work{u + 1}", align_bytes=64) for u in range(2)]
+        h_bf = [keep.tile([P, half * PACK], BF16, name=f"h_bf{u}", align_bytes=64) for u in range(2)]
         h_codes = [keep.tile([P, half], U32, name=f"h_codes{u}", align_bytes=64) for u in range(2)]
         h_bytes = [keep.tile([P, half], U8, name=f"h_bytes{u}", align_bytes=64) for u in range(2)]
         warm = keep.tile([P, 2], F32, name="warm")
         ident = keep.tile([P, P], F32, name="ident")
         cap = keep.tile([P, BLOCKS], F32, name="cap")
+        jump1 = keep.tile([P, BLOCKS], F32, name="jump1")
         jump3 = keep.tile([P, BLOCKS], F32, name="jump3")
         jump3_neg = keep.tile([P, BLOCKS], F32, name="jump3_neg")
 
-        nc.gpsimd.memset(table_scales[:].bitcast(I32), 0)
-        nc.gpsimd.memset(jump_rows[:], 0.0)
+        nc.vector.memset(table_scales[:].bitcast(I32), 0)
+        nc.vector.memset(jump_rows[:], 0.0)
         nc.vector.memset(warm[:, 0:1], 0.0)
         nc.scalar.activation(warm[:, 1:2], warm[:, 0:1], ACT.Exp)
-        for i in range(TILES):
-            nc.gpsimd.memset(prev_t[i][:, PAD - 1 : PAD], FLOAT_MAX)
-            nc.gpsimd.memset(prev_t[i][:, PAD + S : PAD + S + 1], FLOAT_MAX)
         make_identity(nc, ident[:])
-        nc.gpsimd.memset(cap[:, 1 : BLOCKS - 1], FLOAT_MAX)
+        for i in range(TILES):
+            nc.vector.memset(prev_t[i][:, PAD - 1 : PAD], FLOAT_MAX)
+            nc.vector.memset(prev_t[i][:, PAD + S : PAD + S + 1], FLOAT_MAX)
+        nc.vector.memset(cap[:, 1 : BLOCKS - 1], FLOAT_MAX)
         cap_ends = cap[:, 0 : BLOCKS : BLOCKS - 1]
-        nc.gpsimd.tensor_scalar(cap_ends, ident[:, 0 : P : P - 1], -FLOAT_MAX, FLOAT_MAX, ALU.mult, ALU.add)
-        nc.gpsimd.tensor_scalar(cap_ends, cap_ends, 3 * 5.3, 1.0, ALU.add, ALU.mult)
+        nc.vector.tensor_scalar(cap_ends, ident[:, 0 : P : P - 1], -FLOAT_MAX, FLOAT_MAX, ALU.mult, ALU.add)
+        nc.vector.tensor_scalar(cap_ends, cap_ends, 5.3, None, ALU.add)
 
         h_view = hT.rearrange("(p j) w -> p j w", j=PACK)
         scale_rows = x_scales[0].bitcast(I32)
@@ -75,28 +76,35 @@ def tile_picked_ysgm_soft_p_kernel(tc, x_words, x_scales, hT, prev, jump, offs, 
         nc.sync.dma_start(h_raw[0][:], h_view[:, :, 0:half])
         nc.sync.dma_start(jump_rows[0:BLOCKS, :], jump[0, :].rearrange("(c p) -> c p", p=P))
         load_prev(1)
-        load_prev(2)
         nc.sync.dma_start(h_raw[1][:], h_view[:, :, half:V])
+        load_prev(2)
         load_prev(3)
 
         jump_cols = psum.tile([P, S], F32, name="turned")
         nc.tensor.transpose(jump_cols[:, 0:P], jump_rows[:], ident[:])
-        nc.vector.scalar_tensor_tensor(jump3[:], jump_cols[:, 0:BLOCKS], 3.0, cap[:], ALU.mult, ALU.min)
-        nc.scalar.mul(jump3_neg[:], jump3[:], -1.0)
+        nc.vector.tensor_tensor(jump1[:], jump_cols[:, 0:BLOCKS], cap[:], ALU.min)
+        nc.scalar.mul(jump3[:], jump1[:], 3.0)
+        nc.scalar.mul(jump3_neg[:], jump1[:], -3.0)
+        jump_wide = psum.tile([P, S], F32, name="jump_wide", bufs=1)
+        for c in range(BLOCKS):
+            nc.tensor.transpose(jump_wide[:, c * P : (c + 1) * P], jump1[:, c : c + 1].to_broadcast([P, P]), ident[:])
 
         stats = keep.tile([P, 4 * TILES], F32, name="stats")
         sums = keep.tile([P, TILES], F32, name="sums")
-        gain = []
-        base = [keep.tile([P, BLOCKS, half], F32, name=f"base{u}") for u in range(2)]
+        base = []
 
-        def penalty(i):
+        def neighbours(i, negate):
             p = prev_t[i]
-            near = keep.tile([P, S], F32, name=f"near{i}", tag=f"work{i}", align_bytes=64)
+            near = keep.tile([P, S], F32, name=f"near{i}")
             nc.vector.tensor_tensor(near[:], p[:, PAD - 1 : PAD - 1 + S], p[:, PAD + 1 : PAD + 1 + S], ALU.min)
-            neg_mn = stats[:, i : i + 1]
-            nc.vector.tensor_reduce(neg_mn, near[:].rearrange("p (a b) -> p a b", b=4)[:, :, 1:3], AX.XY, ALU.min, negate=True)
+            mn = stats[:, i : i + 1]
+            nc.vector.tensor_reduce(mn, near[:].rearrange("p (a b) -> p a b", b=4)[:, :, 1:3], AX.XY, ALU.min, negate=negate)
             stay = keep.tile([P, S], F32, name=f"stay{i}")
             nc.vector.scalar_tensor_tensor(stay[:], near[:], 0.3, p[:, PAD : PAD + S], ALU.add, ALU.min)
+            return stay, mn
+
+        def turned_gain(i):
+            stay, neg_mn = neighbours(i, True)
             turned = psum.tile([P, S], F32, name="turned")
             for c in range(BLOCKS):
                 cols = slice(c * P, (c + 1) * P)
@@ -108,60 +116,96 @@ def tile_picked_ysgm_soft_p_kernel(tc, x_words, x_scales, hT, prev, jump, offs, 
             for c in range(BLOCKS):
                 cols = slice(c * P, (c + 1) * P)
                 nc.scalar.activation(w[:, cols], turned[:, cols], ACT.Relu, bias=jump3[:, c : c + 1], scale=-3.0)
-            gain.append(w)
+            return w
 
-        def product(u):
+        def quantise(u):
             nc.scalar.copy(
                 h_bf[u][:].rearrange("p (c i t) -> p c t i", i=4, t=PACK),
                 h_raw[u][:].rearrange("p t (c i) -> p c t i", i=4),
             )
             nc.vector.quantize_mx(out=h_codes[u][:].bitcast(FP8X4), scales=h_bytes[u][:], in_=h_bf[u][:])
-            for pair in range(BLOCKS // 2):
-                acc = psum.tile([P, 2, half], F32, name="acc", bufs=2)
-                for d in range(2):
-                    c = 2 * pair + d
+
+        def turned_product(u, width):
+            per_bank = S // width
+            base.append(keep.tile([P, BLOCKS, width], F32, name=f"base{u}"))
+            for first in range(0, BLOCKS, per_bank):
+                acc = psum.tile([P, per_bank, width], F32, name="acc")
+                for d in range(per_bank):
+                    c = first + d
                     nc.tensor.matmul_mx(
                         out=acc[:, d, :],
                         lhsT=x_codes[:, c * P : (c + 1) * P].bitcast(FP8X4),
                         lhsT_scale=x_bytes[:, c * P : (c + 1) * P],
-                        rhs=h_codes[u][:].bitcast(FP8X4),
-                        rhs_scale=h_bytes[u][:],
+                        rhs=h_codes[u][:, 0:width].bitcast(FP8X4),
+                        rhs_scale=h_bytes[u][:, 0:width],
                         start=True,
                         stop=True,
                     )
-                for d in range(2):
-                    c = 2 * pair + d
+                for d in range(per_bank):
+                    c = first + d
                     nc.scalar.activation(base[u][:, c, :], acc[:, d, :], ACT.Identity, bias=jump3_neg[:, c : c + 1], scale=0.9)
 
-        def finish(i):
+        def softmax(i, logits, scale, shift):
+            e = keep.tile([P, S], F32, name=f"e{i}")
+            nc.scalar.activation(e[:], logits, ACT.Exp, bias=shift, scale=scale, accum_out=sums[:, i : i + 1])
+            r = stats[:, 2 * TILES + i : 2 * TILES + i + 1]
+            nc.vector.reciprocal(r, sums[:, i : i + 1])
+            o = keep.tile([P, S], F32, name=f"o{i}")
+            if i >= 2:
+                for cols in (slice(0, S // 2), slice(S // 2, S)):
+                    nc.vector.tensor_scalar(o[:, cols], e[:, cols], r, None, ALU.mult)
+                    nc.sync.dma_start(out[i * P : (i + 1) * P, cols], o[:, cols])
+            else:
+                nc.gpsimd.tensor_scalar(o[:], e[:], r, 1.0, ALU.mult, ALU.mult)
+                nc.sync.dma_start(out[i * P : (i + 1) * P, :], o[:])
+
+        def turned_logits(i, gain):
             u, d = divmod(i, 2)
-            z = psum.tile([P, S], F32, name="z", bufs=4)
+            z = psum.tile([P, S], F32, name="z", bufs=3)
             for c in range(BLOCKS):
                 cols = slice(c * P, (c + 1) * P)
                 nc.tensor.matmul(z[:, cols], base[u][:, c, d * P : (d + 1) * P], ident[:], start=(c == 0), stop=False, is_transpose=True)
             for c in range(BLOCKS):
                 cols = slice(c * P, (c + 1) * P)
-                nc.tensor.matmul(z[:, cols], gain[i][:, cols], ident[:], start=False, stop=(c == BLOCKS - 1), is_transpose=True)
+                nc.tensor.matmul(z[:, cols], gain[:, cols], ident[:], start=False, stop=(c == BLOCKS - 1), is_transpose=True)
+            return z
+
+        def turned_softmax(i, z):
             neg_max = stats[:, TILES + i : TILES + i + 1]
             nc.vector.tensor_reduce(neg_max, z[:], AX.X, ALU.max, negate=True)
-            e = keep.tile([P, S], F32, name=f"e{i}")
-            nc.scalar.activation(e[:], z[:], ACT.Exp, bias=neg_max, accum_out=sums[:, i : i + 1])
-            r = stats[:, 2 * TILES + i : 2 * TILES + i + 1]
-            nc.vector.reciprocal(r, sums[:, i : i + 1])
-            o = keep.tile([P, S], F32, name=f"o{i}")
-            if i == TILES - 1:
-                nc.vector.tensor_scalar(o[:], e[:], r, None, ALU.mult)
-            else:
-                nc.gpsimd.tensor_scalar(o[:], e[:], r, 1.0, ALU.mult, ALU.mult)
-            nc.sync.dma_start(out[i * P : (i + 1) * P, :], o[:])
+            softmax(i, z[:], 1.0, neg_max)
 
-        penalty(0)
+        gain0 = turned_gain(0)
         nc.vector.tensor_copy(x_codes[:], table_words[:].indirect(offsets[:]))
         nc.vector.tensor_copy(x_bytes[:], table_scales[:].indirect(offsets[:]))
-        product(0)
-        penalty(1)
-        product(1)
-        penalty(2)
-        penalty(3)
-        for i in range(TILES):
-            finish(i)
+        quantise(0)
+        quantise(1)
+        turned_product(0, half)
+        gain1 = turned_gain(1)
+        turned_product(1, P)
+        acc3 = psum.tile([P, S], F32, name="acc")
+        nc.tensor.matmul_mx(
+            out=acc3[:],
+            lhsT=h_codes[1][:, P:half].bitcast(FP8X4),
+            lhsT_scale=h_bytes[1][:, P:half],
+            rhs=x_codes[:].bitcast(FP8X4),
+            rhs_scale=x_bytes[:],
+            start=True,
+            stop=True,
+        )
+        z0 = turned_logits(0, gain0)
+        gain2 = turned_gain(2)
+        z1 = turned_logits(1, gain1)
+        stay3, mn3 = neighbours(3, False)
+        turned_softmax(0, z0)
+        pen3 = keep.tile([P, S], F32, name="pen3")
+        nc.vector.scalar_tensor_tensor(pen3[:], stay3[:], mn3, jump_wide[:], ALU.subtract, ALU.min)
+        turned_softmax(1, z1)
+        z3 = keep.tile([P, S], F32, name="z3")
+        nc.vector.scalar_tensor_tensor(z3[:], acc3[:], 0.3, pen3[:], ALU.mult, ALU.subtract)
+        z2 = turned_logits(2, gain2)
+        turned_softmax(2, z2)
+        cost3 = keep.tile([P, S], F32, name="cost3")
+        low3 = stats[:, TILES + 3 : TILES + 4]
+        nc.vector.tensor_scalar(cost3[:], z3[:], -3.0, None, ALU.mult, ALU.min, accum_out=low3)
+        softmax(3, cost3[:], -1.0, low3)

from contextlib import ExitStack

import concourse.mybir as mybir
from concourse.masks import make_identity

K, T, S, V = 512, 1024, 512, 512
P = 128
PACK = 4
TILES = V // P
BLOCKS = S // P
PAD = 8
FLOPS = 2 * K * S * V
FLOAT_MAX = 3.4028234663852886e38

F32 = mybir.dt.float32
BF16 = mybir.dt.bfloat16
I32 = mybir.dt.int32
U32 = mybir.dt.uint32
U16 = mybir.dt.uint16
U8 = mybir.dt.uint8
FP8X4 = mybir.dt.float8_e4m3fn_x4
ALU = mybir.AluOpType
ACT = mybir.ActivationFunctionType
AX = mybir.AxisListType


def tile_picked_ysgm_soft_p_kernel(tc, x_words, x_scales, hT, prev, jump, offs, out):
    nc = tc.nc
    with ExitStack() as ctx:
        keep = ctx.enter_context(tc.tile_pool(name="keep", bufs=1))
        psum = ctx.enter_context(tc.psum_pool(name="psum", bufs=2))

        offsets = keep.tile([P, S // 16], U16, name="offsets")
        table_words = keep.tile([P, T], U32, name="table_words", align_bytes=64)
        table_scales = keep.tile([P, T], U8, name="table_scales", align_bytes=64)
        x_codes = keep.tile([P, S], U32, name="x_codes", align_bytes=64)
        x_bytes = keep.tile([P, S], U8, name="x_bytes", align_bytes=64)
        prev_t = [keep.tile([P, S + 2 * PAD], F32, name=f"prev{i}") for i in range(TILES)]
        jump_rows = keep.tile([P, P], F32, name="jump_rows")
        half = V // 2
        h_raw = [keep.tile([P, PACK, half], F32, name=f"h_raw{u}") for u in range(2)]
        h_bf = [keep.tile([P, half * PACK], BF16, name=f"h_bf{u}", align_bytes=64) for u in range(2)]
        h_codes = [keep.tile([P, half], U32, name=f"h_codes{u}", align_bytes=64) for u in range(2)]
        h_bytes = [keep.tile([P, half], U8, name=f"h_bytes{u}", align_bytes=64) for u in range(2)]
        warm = keep.tile([P, 2], F32, name="warm")
        ident = keep.tile([P, P], F32, name="ident")
        cap = keep.tile([P, BLOCKS], F32, name="cap")
        jump1 = keep.tile([P, BLOCKS], F32, name="jump1")
        jump3 = keep.tile([P, BLOCKS], F32, name="jump3")
        jump3_neg = keep.tile([P, BLOCKS], F32, name="jump3_neg")

        nc.vector.memset(table_scales[:].bitcast(I32), 0)
        nc.vector.memset(jump_rows[:], 0.0)
        nc.vector.memset(warm[:, 0:1], 0.0)
        nc.scalar.activation(warm[:, 1:2], warm[:, 0:1], ACT.Exp)
        make_identity(nc, ident[:])
        for i in range(TILES):
            nc.vector.memset(prev_t[i][:, PAD - 1 : PAD], FLOAT_MAX)
            nc.vector.memset(prev_t[i][:, PAD + S : PAD + S + 1], FLOAT_MAX)
        nc.vector.memset(cap[:, 1 : BLOCKS - 1], FLOAT_MAX)
        cap_ends = cap[:, 0 : BLOCKS : BLOCKS - 1]
        nc.vector.tensor_scalar(cap_ends, ident[:, 0 : P : P - 1], -FLOAT_MAX, FLOAT_MAX, ALU.mult, ALU.add)
        nc.vector.tensor_scalar(cap_ends, cap_ends, 5.3, None, ALU.add)

        h_view = hT.rearrange("(p j) w -> p j w", j=PACK)
        scale_rows = x_scales[0].bitcast(I32)

        def load_prev(i):
            nc.sync.dma_start(prev_t[i][:, PAD : PAD + S], prev[i * P : (i + 1) * P, :])

        load_prev(0)
        nc.sync.dma_start(offsets[:], offs)
        nc.sync.dma_start(table_words[:].bitcast(I32), x_words[0].rearrange("p n t -> p (n t)").bitcast(I32))
        for q in range(4):
            nc.sync.dma_start(table_scales[32 * q : 32 * q + 4, :].bitcast(I32), scale_rows[4 * q : 4 * q + 4, :])
        nc.sync.dma_start(h_raw[0][:], h_view[:, :, 0:half])
        nc.sync.dma_start(jump_rows[0:BLOCKS, :], jump[0, :].rearrange("(c p) -> c p", p=P))
        load_prev(1)
        nc.sync.dma_start(h_raw[1][:], h_view[:, :, half:V])
        load_prev(2)
        load_prev(3)

        jump_cols = psum.tile([P, S], F32, name="turned")
        nc.tensor.transpose(jump_cols[:, 0:P], jump_rows[:], ident[:])
        nc.vector.tensor_tensor(jump1[:], jump_cols[:, 0:BLOCKS], cap[:], ALU.min)
        nc.scalar.mul(jump3[:], jump1[:], 3.0)
        nc.scalar.mul(jump3_neg[:], jump1[:], -3.0)
        jump_wide = psum.tile([P, S], F32, name="jump_wide", bufs=1)
        for c in range(BLOCKS):
            nc.tensor.transpose(jump_wide[:, c * P : (c + 1) * P], jump1[:, c : c + 1].to_broadcast([P, P]), ident[:])

        stats = keep.tile([P, 4 * TILES], F32, name="stats")
        sums = keep.tile([P, TILES], F32, name="sums")
        base = []

        def neighbours(i, negate):
            p = prev_t[i]
            near = keep.tile([P, S], F32, name=f"near{i}")
            nc.vector.tensor_tensor(near[:], p[:, PAD - 1 : PAD - 1 + S], p[:, PAD + 1 : PAD + 1 + S], ALU.min)
            mn = stats[:, i : i + 1]
            nc.vector.tensor_reduce(mn, near[:].rearrange("p (a b) -> p a b", b=4)[:, :, 1:3], AX.XY, ALU.min, negate=negate)
            stay = keep.tile([P, S], F32, name=f"stay{i}")
            nc.vector.scalar_tensor_tensor(stay[:], near[:], 0.3, p[:, PAD : PAD + S], ALU.add, ALU.min)
            return stay, mn

        def turned_gain(i):
            stay, neg_mn = neighbours(i, True)
            turned = psum.tile([P, S], F32, name="turned")
            for c in range(BLOCKS):
                cols = slice(c * P, (c + 1) * P)
                nc.tensor.matmul(turned[:, cols], neg_mn.to_broadcast([P, P]), ident[:], start=(c == 0), stop=False, is_transpose=True)
            for c in range(BLOCKS):
                cols = slice(c * P, (c + 1) * P)
                nc.tensor.matmul(turned[:, cols], stay[:, cols], ident[:], start=False, stop=(c == BLOCKS - 1), is_transpose=True)
            w = keep.tile([P, S], F32, name=f"gain{i}")
            for c in range(BLOCKS):
                cols = slice(c * P, (c + 1) * P)
                nc.scalar.activation(w[:, cols], turned[:, cols], ACT.Relu, bias=jump3[:, c : c + 1], scale=-3.0)
            return w

        def quantise(u):
            nc.scalar.copy(
                h_bf[u][:].rearrange("p (c i t) -> p c t i", i=4, t=PACK),
                h_raw[u][:].rearrange("p t (c i) -> p c t i", i=4),
            )
            nc.vector.quantize_mx(out=h_codes[u][:].bitcast(FP8X4), scales=h_bytes[u][:], in_=h_bf[u][:])

        def turned_product(u, width):
            per_bank = S // width
            base.append(keep.tile([P, BLOCKS, width], F32, name=f"base{u}"))
            for first in range(0, BLOCKS, per_bank):
                acc = psum.tile([P, per_bank, width], F32, name="acc")
                for d in range(per_bank):
                    c = first + d
                    nc.tensor.matmul_mx(
                        out=acc[:, d, :],
                        lhsT=x_codes[:, c * P : (c + 1) * P].bitcast(FP8X4),
                        lhsT_scale=x_bytes[:, c * P : (c + 1) * P],
                        rhs=h_codes[u][:, 0:width].bitcast(FP8X4),
                        rhs_scale=h_bytes[u][:, 0:width],
                        start=True,
                        stop=True,
                    )
                for d in range(per_bank):
                    c = first + d
                    nc.scalar.activation(base[u][:, c, :], acc[:, d, :], ACT.Identity, bias=jump3_neg[:, c : c + 1], scale=0.9)

        def softmax(i, logits, scale, shift):
            e = keep.tile([P, S], F32, name=f"e{i}")
            nc.scalar.activation(e[:], logits, ACT.Exp, bias=shift, scale=scale, accum_out=sums[:, i : i + 1])
            r = stats[:, 2 * TILES + i : 2 * TILES + i + 1]
            nc.vector.reciprocal(r, sums[:, i : i + 1])
            o = keep.tile([P, S], F32, name=f"o{i}")
            if i >= 2:
                for cols in (slice(0, S // 2), slice(S // 2, S)):
                    nc.vector.tensor_scalar(o[:, cols], e[:, cols], r, None, ALU.mult)
                    nc.sync.dma_start(out[i * P : (i + 1) * P, cols], o[:, cols])
            else:
                nc.gpsimd.tensor_scalar(o[:], e[:], r, 1.0, ALU.mult, ALU.mult)
                nc.sync.dma_start(out[i * P : (i + 1) * P, :], o[:])

        def turned_logits(i, gain):
            u, d = divmod(i, 2)
            z = psum.tile([P, S], F32, name="z", bufs=3)
            for c in range(BLOCKS):
                cols = slice(c * P, (c + 1) * P)
                nc.tensor.matmul(z[:, cols], base[u][:, c, d * P : (d + 1) * P], ident[:], start=(c == 0), stop=False, is_transpose=True)
            for c in range(BLOCKS):
                cols = slice(c * P, (c + 1) * P)
                nc.tensor.matmul(z[:, cols], gain[:, cols], ident[:], start=False, stop=(c == BLOCKS - 1), is_transpose=True)
            return z

        def turned_softmax(i, z):
            neg_max = stats[:, TILES + i : TILES + i + 1]
            nc.vector.tensor_reduce(neg_max, z[:], AX.X, ALU.max, negate=True)
            softmax(i, z[:], 1.0, neg_max)

        gain0 = turned_gain(0)
        nc.vector.tensor_copy(x_codes[:], table_words[:].indirect(offsets[:]))
        nc.vector.tensor_copy(x_bytes[:], table_scales[:].indirect(offsets[:]))
        quantise(0)
        quantise(1)
        turned_product(0, half)
        gain1 = turned_gain(1)
        turned_product(1, P)
        acc3 = psum.tile([P, S], F32, name="acc")
        nc.tensor.matmul_mx(
            out=acc3[:],
            lhsT=h_codes[1][:, P:half].bitcast(FP8X4),
            lhsT_scale=h_bytes[1][:, P:half],
            rhs=x_codes[:].bitcast(FP8X4),
            rhs_scale=x_bytes[:],
            start=True,
            stop=True,
        )
        z0 = turned_logits(0, gain0)
        gain2 = turned_gain(2)
        z1 = turned_logits(1, gain1)
        stay3, mn3 = neighbours(3, False)
        turned_softmax(0, z0)
        pen3 = keep.tile([P, S], F32, name="pen3")
        nc.vector.scalar_tensor_tensor(pen3[:], stay3[:], mn3, jump_wide[:], ALU.subtract, ALU.min)
        turned_softmax(1, z1)
        z3 = keep.tile([P, S], F32, name="z3")
        nc.vector.scalar_tensor_tensor(z3[:], acc3[:], 0.3, pen3[:], ALU.mult, ALU.subtract)
        z2 = turned_logits(2, gain2)
        turned_softmax(2, z2)
        cost3 = keep.tile([P, S], F32, name="cost3")
        low3 = stats[:, TILES + 3 : TILES + 4]
        nc.vector.tensor_scalar(cost3[:], z3[:], -3.0, None, ALU.mult, ALU.min, accum_out=low3)
        softmax(3, cost3[:], -1.0, low3)
